import numpy as np
import ml_dtypes


def mxq(x, axis, fmt="e4m3"):
    dtype, down = {"e4m3": (ml_dtypes.float8_e4m3fn, 7), "e5m2": (ml_dtypes.float8_e5m2, 14)}[fmt]
    v = np.moveaxis(np.asarray(x, np.float32).astype(ml_dtypes.bfloat16).astype(np.float64), axis, -1)
    blocks = v.reshape(v.shape[:-1] + (-1, 32))
    amax = np.abs(blocks).max(-1, keepdims=True)
    byte = np.maximum(np.where(amax > 0, np.frexp(amax)[1] - 1 + 127, 0) - down, 1)
    scale = np.exp2(byte - 127.0)
    codes = (blocks / scale).astype(np.float32).astype(dtype).astype(np.float64)
    return np.moveaxis((codes * scale).reshape(v.shape), -1, axis)


WIDE = False


def mx_kscale(k):
    if not WIDE:
        return np.ones(k)
    levels = np.array([10, -10, 5, -5, 0])
    if k % 512:
        return np.exp2(np.random.permutation(np.resize(levels, k // 32))).repeat(32)
    a = np.empty((k // 512, 16))
    for p in range(k // 512):
        a[p, :8] = np.random.permutation(np.resize(levels, 8))
        for g in range(8):
            far = levels[np.abs(levels - a[p, g]) >= 10]
            a[p, g + 8] = far[np.random.randint(len(far))]
    return np.exp2(a.ravel()).repeat(32)


def f64(x):
    return np.asarray(x).astype(np.float64)


def striped(idx):
    return np.tile(idx.reshape(-1, 16).T, (8, 1)).astype(np.uint16)


def unstriped(offs):
    return offs[:16].T.reshape(-1).astype(np.int64)


E2M1 = np.array([0.0, 0.5, 1.0, 1.5, 2.0, 3.0, 4.0, 6.0, -0.0, -0.5, -1.0, -1.5, -2.0, -3.0, -4.0, -6.0])


def pack_weight(w, fmt):
    k, n = w.shape
    w = f64(np.asarray(w, np.float32).astype(ml_dtypes.bfloat16)).reshape(k // 32, 32, n)
    amax = np.abs(w).max(1)
    if fmt == "e4m3":
        byte = np.frexp(amax)[1] - 1 + 127 - 7
    else:
        mant, ex = np.frexp(amax / 6.0)
        byte = np.where(mant > 0.5, ex, ex - 1) + 127
    byte = np.clip(np.where(amax > 0, byte, 1), 1, 254)
    scaled = (w * np.exp2(127.0 - byte)[:, None, :]).reshape(k, n).astype(np.float32)
    by_word = np.ascontiguousarray(scaled.reshape(k // 512, 128, 4, n).transpose(0, 1, 3, 2))
    if fmt == "e4m3":
        words = by_word.astype(ml_dtypes.float8_e4m3fn).view(np.uint8)
    else:
        c = by_word.astype(ml_dtypes.float4_e2m1fn).view(np.uint8) & 0xF
        words = (c[..., 0::2] | (c[..., 1::2] << 4)).reshape(k // 512, 128, 2 * n)
    return np.ascontiguousarray(words), np.ascontiguousarray(byte.astype(np.uint8).reshape(k // 512, 16, n))


def unpack_weight(words, scales, fmt):
    g, _, n = scales.shape
    words = np.ascontiguousarray(words).reshape(g, 128, n, -1)
    if fmt == "e4m3":
        vals = words.view(ml_dtypes.float8_e4m3fn).astype(np.float64)
    else:
        nib = np.empty((g, 128, n, 4), np.uint8)
        nib[..., 0::2] = words & 0xF
        nib[..., 1::2] = words >> 4
        vals = E2M1[nib]
    vals = vals * np.repeat(np.exp2(scales.astype(np.float64) - 127.0), 8, axis=1)[..., None]
    return vals.transpose(0, 1, 3, 2).reshape(g * 512, n)


def gelu(v):
    return 0.5 * v * (1.0 + np.tanh(np.sqrt(2.0 / np.pi) * (v + 0.044715 * v**3)))


K, H, N, T, S, T2 = 1024, 1024, 256, 2048, 512, 1024

def setup_inputs():
    n = np.random.standard_normal
    s, u = mx_kscale(K)[:, None], mx_kscale(H)[:, None]
    tab_words, tab_scales = pack_weight(n((K, T)) * s, "e4m3")
    w1 = (0.15 * n((K, H)) / np.sqrt(K) / s).astype(np.float32)
    w2_words, w2_scales = pack_weight(0.15 * n((K, H)) / np.sqrt(K) / s, "e2m1")
    w3 = (n((H, N)) / np.sqrt(H) / u).astype(np.float32)
    w4_words, w4_scales = pack_weight(n((H, N)) / np.sqrt(H) / u, "e4m3")
    return {
        "tab_words": tab_words, "tab_scales": tab_scales,
        "offs": striped(np.random.permutation(T)[:S]),
        "offs2": striped(np.random.permutation(T2)[:S]),
        "offs3": striped(np.random.permutation(T2)[:S]),
        "w1": w1, "w2_words": w2_words, "w2_scales": w2_scales,
        "wg1": np.exp(0.3 * n((128, S))).astype(np.float32),
        "wg2": np.exp(0.3 * n((128, S))).astype(np.float32),
        "delay": np.random.uniform(-1.3, 1.3, (H, T2)).astype(np.float32),
        "tune": (np.random.uniform(0.5, 1.5, H) * u[:, 0]).astype(np.float32),
        "loud": (np.random.uniform(2.0, 5.0, H) * u[:, 0]).astype(np.float32),
        "w3": w3, "w4_words": w4_words, "w4_scales": w4_scales,
    }

def reference(tab_words, tab_scales, offs, offs2, offs3, w1, w2_words, w2_scales,
              wg1, wg2, delay, tune, loud, w3, w4_words, w4_scales):
    v = unpack_weight(tab_words, tab_scales, "e4m3")[:, unstriped(offs)]
    h1 = mxq(f64(w1), 0, "e4m3").T @ v
    h2 = unpack_weight(w2_words, w2_scales, "e2m1").T @ v
    pageA = np.zeros((H, T2))
    pageA[:, unstriped(offs2)] = np.tile(f64(wg1), (H // 128, 1)) * h1
    pageB = np.zeros((H, T2))
    pageB[:, unstriped(offs3)] = np.tile(f64(wg2), (H // 128, 1)) * h2
    z = np.cos(pageA - pageB + f64(delay)) * f64(tune)[:, None]
    left = pageA * f64(loud)[:, None]
    both = mxq(f64(w3), 0, "e4m3").T @ mxq(z, 0, "e4m3")
    alone = unpack_weight(w4_words, w4_scales, "e4m3").T @ mxq(left, 0, "e4m3")
    out = both + alone
    return out

@@ -1,0 +1,340 @@
+import math
+from contextlib import ExitStack
+
+import concourse.mybir as mybir
+from concourse.masks import make_identity
+
+K, H, N, T, S, T2 = 1024, 1024, 256, 2048, 512, 1024
+FLOPS = 2 * (2 * K * H * S + 2 * H * N * T2)
+
+F32 = mybir.dt.float32
+BF16 = mybir.dt.bfloat16
+I32 = mybir.dt.int32
+U32 = mybir.dt.uint32
+U16 = mybir.dt.uint16
+U8 = mybir.dt.uint8
+FP8X4 = mybir.dt.float8_e4m3fn_x4
+FP4X4 = mybir.dt.float4_e2m1fn_x4
+MULT = mybir.AluOpType.mult
+ACT = mybir.ActivationFunctionType
+
+P = 128
+PACK = 4
+PASS = P * PACK
+PASSES = 2
+BANK = 512
+AHEAD = 4
+
+
+def tile_list_owl_phase_cosine_kernel(tc, tab_words, tab_scales, offs, offs2, offs3, w1, w2_words, w2_scales,
+                                                wg1, wg2, delay, tune, loud, w3, w4_words, w4_scales, out):
+    nc = tc.nc
+    with ExitStack() as ctx:
+        keep = ctx.enter_context(tc.tile_pool(name="keep", bufs=1))
+        psum = ctx.enter_context(tc.psum_pool(name="psum", bufs=1))
+
+        def load_scale_rows(plane, scales):
+            rows = scales.bitcast(I32)
+            for q in range(4):
+                nc.sync.dma_start(out=plane[32 * q:32 * q + 4, :, :].bitcast(I32),
+                                  in_=rows[:, 4 * q:4 * q + 4, :].rearrange("a r w -> r a w"))
+
+        def load_gains(gains, wg, pair):
+            cols = slice(2 * S * pair, 2 * S * (pair + 1))
+            rows = wg.rearrange("(q t) j -> q (t j)", t=PACK)[:, cols]
+            for q in range(4):
+                nc.sync.dma_start(out=gains[32 * q:32 * q + 32, cols], in_=rows)
+
+        grain_list = keep.tile([P, S // 16], U16)
+        left_list = keep.tile([P, S // 16], U16)
+        right_list = keep.tile([P, S // 16], U16)
+        tab_plane = keep.tile([P, PASSES, T], U8, align_bytes=64)
+        w2_plane_raw = keep.tile([P, PASSES, H], U8, align_bytes=64)
+        w4_plane = keep.tile([P, PASSES, N], U8, align_bytes=64)
+        w2_raw = [keep.tile([P, PASSES, 2 * PASS], U8, name="w2_raw%d" % b, align_bytes=64) for b in range(PASSES)]
+        tab = [keep.tile([P, T], U32, name="tab%d" % a, align_bytes=64) for a in range(PASSES)]
+        gain_right = keep.tile([P, PACK * S], F32)
+        gain_left = keep.tile([P, PACK * S], F32)
+        tune_col = keep.tile([P, PASSES, PACK], F32)
+        loud_col = keep.tile([P, PASSES, PACK], F32)
+        stage = [keep.tile([P, PACK * PASS], F32, name="stage%d" % i) for i in range(3)]
+        spare = keep.tile([P, 2 * S], F32)
+        cosine = [keep.tile([P, PACK * T2], F32, name="cosine%d" % b) for b in range(PASSES)]
+        delay_rows = [keep.tile([P, T2], F32, name="delay_rows%d" % t) for t in range(PACK)]
+        page_right = [keep.tile([P, T2], F32, name="page_right%d" % t) for t in range(PACK)]
+        page_left = [keep.tile([P, T2], F32, name="page_left%d" % t) for t in range(PACK)]
+        ident = keep.tile([P, P], F32)
+        grain_codes = [keep.tile([P, S], U32, name="grain_codes%d" % a, align_bytes=64) for a in range(PASSES)]
+        grain_plane = [keep.tile([P, S], U8, name="grain_plane%d" % a, align_bytes=64) for a in range(PASSES)]
+        w2_codes = [keep.tile([P, PASSES, 2 * PASS], U8, name="w2_codes%d" % b, align_bytes=64) for b in range(PASSES)]
+        w2_plane = [keep.tile([P, PASSES, PASS], U8, name="w2_plane%d" % b, align_bytes=64) for b in range(PASSES)]
+        grouped = [keep.tile([P, PACK * PASS], BF16, name="grouped%d" % a, align_bytes=64) for a in range(PASSES)]
+        w1_codes = {(a, b): keep.tile([P, PASS], U32, name="w1_codes%d%d" % (a, b), align_bytes=64)
+                    for a in range(PASSES) for b in range(PASSES)}
+        w1_plane = {(a, b): keep.tile([P, PASS], U8, name="w1_plane%d%d" % (a, b), align_bytes=64)
+                    for a in range(PASSES) for b in range(PASSES)}
+        w3_codes = keep.tile([P, PASSES * N], U32, align_bytes=64)
+        w3_plane = keep.tile([P, PASSES * N], U8, align_bytes=64)
+        w4_codes = keep.tile([P, PASSES, N], U32, align_bytes=64)
+        left_rows = keep.tile([P, PACK * T2], BF16)
+        woven_left = keep.tile([P, PACK * T2], BF16, align_bytes=64)
+        woven_z = keep.tile([P, PACK * T2], BF16, align_bytes=64)
+        left_codes = [keep.tile([P, T2], U32, name="left_codes%d" % b, align_bytes=64) for b in range(PASSES)]
+        left_plane = [keep.tile([P, T2], U8, name="left_plane%d" % b, align_bytes=64) for b in range(PASSES)]
+        z_codes = [keep.tile([P, T2], U32, name="z_codes%d" % b, align_bytes=64) for b in range(PASSES)]
+        z_plane = [keep.tile([P, T2], U8, name="z_plane%d" % b, align_bytes=64) for b in range(PASSES)]
+        warm = keep.tile([P, 1], F32)
+        bank = [psum.tile([P, BANK], F32, name="bank%d" % i) for i in range(8)]
+
+        w1_raw = {(0, 0): stage[0][:], (1, 0): stage[1][:], (0, 1): cosine[1][:, 0:PACK * PASS], (1, 1): stage[2][:]}
+        w3_raw = cosine[1][:, PACK * PASS:2 * PACK * PASS]
+
+        def slot(tile, i):
+            return tile[:, S * i:S * (i + 1)]
+
+        h_slot = ([slot(spare, 0), slot(spare, 1)] + [slot(stage[1], i) for i in range(3)]
+                  + [slot(stage[2], i) for i in range(3)] + [slot(stage[0], i) for i in range(4)]
+                  + [slot(stage[1], 3), slot(stage[2], 3), slot(spare, 0), woven_z[:, 6 * BANK:8 * BANK].bitcast(F32)])
+        result_slot = [slot(stage[0], i) for i in range(4)]
+
+        nc.vector.memset(tab_plane[:].bitcast(I32), 0)
+        nc.vector.memset(w2_plane_raw[:].bitcast(I32), 0)
+        nc.vector.memset(warm[:], 0.0)
+        nc.scalar.activation(out=warm[:], in_=warm[:], func=ACT.Sin)
+        for t in range(PACK):
+            nc.gpsimd.memset(page_right[t][:], 0.0)
+        make_identity(nc, ident[:])
+        for t in range(PACK):
+            nc.gpsimd.memset(page_left[t][:], 0.0)
+        nc.gpsimd.memset(w4_plane[:].bitcast(I32), 0)
+
+        def load_w1(a, b):
+            nc.sync.dma_start(out=w1_raw[(a, b)].rearrange("p (j c) -> p j c", j=PACK),
+                              in_=w1[PASS * a:PASS * (a + 1), PASS * b:PASS * (b + 1)].rearrange(
+                                  "(p j) c -> p j c", j=PACK))
+
+        def load_delay(b, t):
+            nc.sync.dma_start(out=delay_rows[t][:], in_=delay[PASS * b:PASS * (b + 1), :].rearrange(
+                "(p t) m -> p t m", t=PACK)[:, t, :])
+
+        def load_w2(b):
+            nc.sync.dma_start(out=w2_raw[b][:].bitcast(I32),
+                              in_=w2_words[:, :, 2 * PASS * b:2 * PASS * (b + 1)].bitcast(I32).rearrange("a p w -> p a w"))
+
+        nc.sync.dma_start(grain_list[:], offs)
+        load_scale_rows(tab_plane, tab_scales)
+        load_w2(0)
+        load_scale_rows(w2_plane_raw, w2_scales)
+        for a in range(PASSES):
+            nc.sync.dma_start(out=tab[a][:].bitcast(I32),
+                              in_=tab_words[a].rearrange("p t i -> p (t i)").bitcast(I32))
+        load_w2(1)
+        nc.sync.dma_start(right_list[:], offs3)
+        load_gains(gain_right, wg2, 0)
+        for a in range(PASSES):
+            load_w1(a, 0)
+        load_gains(gain_right, wg2, 1)
+        load_w1(0, 1)
+        nc.sync.dma_start(left_list[:], offs2)
+        load_gains(gain_left, wg1, 0)
+        load_w1(1, 1)
+        nc.sync.dma_start(out=loud_col[:], in_=loud.rearrange("(a p t) -> p a t", a=PASSES, t=PACK))
+        load_delay(0, 0)
+        load_gains(gain_left, wg1, 1)
+        for t in range(1, PACK):
+            load_delay(0, t)
+        for a in range(PASSES):
+            nc.sync.dma_start(
+                out=w3_raw[:, PACK * N * a:PACK * N * (a + 1)].rearrange("p (j n) -> p j n", j=PACK),
+                in_=w3[PASS * a:PASS * (a + 1), :].rearrange("(p j) n -> p j n", j=PACK))
+        nc.sync.dma_start(out=tune_col[:], in_=tune.rearrange("(a p t) -> p a t", a=PASSES, t=PACK))
+        nc.sync.dma_start(out=w4_codes[:].bitcast(I32), in_=w4_words.rearrange("a p c i -> p a (c i)").bitcast(I32))
+        load_scale_rows(w4_plane, w4_scales)
+
+        def order_w2(b):
+            nc.vector.tensor_copy(
+                out=w2_codes[b][:].bitcast(U16).rearrange("p a (t m) -> p a t m", t=PACK),
+                in_=w2_raw[b][:].bitcast(U16).rearrange("p a (m t) -> p a t m", t=PACK))
+            nc.vector.tensor_copy(
+                out=w2_plane[b][:].rearrange("p a (t m) -> p a t m", t=PACK),
+                in_=w2_plane_raw[:, :, PASS * b:PASS * (b + 1)].rearrange("p a (m t) -> p a t m", t=PACK))
+
+        for a in range(PASSES):
+            nc.vector.tensor_copy(grain_plane[a][:], tab_plane[:, a, :].indirect(grain_list[:]))
+        order_w2(0)
+        for a in range(PASSES):
+            nc.vector.tensor_copy(grain_codes[a][:], tab[a][:].indirect(grain_list[:]))
+        order_w2(1)
+
+        def quantise_w1(a, b):
+            nc.scalar.copy(out=grouped[a][:].rearrange("p (t m j) -> p m t j", t=PACK, j=PACK),
+                           in_=w1_raw[(a, b)].rearrange("p (j m t) -> p m t j", j=PACK, t=PACK))
+            nc.vector.quantize_mx(out=w1_codes[(a, b)][:].bitcast(FP8X4), scales=w1_plane[(a, b)][:], in_=grouped[a][:])
+
+        def quantise_w3():
+            for a in range(PASSES):
+                cols = slice(PACK * N * a, PACK * N * (a + 1))
+                nc.scalar.copy(out=woven_z[:, cols].rearrange("p (c i j) -> p c j i", i=4, j=PACK),
+                               in_=w3_raw[:, cols].rearrange("p (j c i) -> p c j i", j=PACK, i=4))
+            nc.vector.quantize_mx(out=w3_codes[:].bitcast(FP8X4), scales=w3_plane[:], in_=woven_z[:, 0:PACK * PASSES * N])
+
+        phase_bank = [0, 1, 0, 1, 1, 0, 6, 1, 7, 0, 6, 1, 4, 5, 4, 5]
+
+        def phases(step):
+            ear, b, t = steps[step]
+            acc = bank[phase_bank[step]]
+            cols = slice(P * t, P * (t + 1))
+            for a in range(PASSES):
+                if ear == "left":
+                    lhs, lhs_plane = w1_codes[(a, b)][:, cols].bitcast(FP8X4), w1_plane[(a, b)][:, cols]
+                else:
+                    lhs = w2_codes[b][:, a, 2 * P * t:2 * P * (t + 1)].bitcast(FP4X4)
+                    lhs_plane = w2_plane[b][:, a, cols]
+                nc.tensor.matmul_mx(out=acc[:], lhsT=lhs, lhsT_scale=lhs_plane,
+                                    rhs=grain_codes[a][:].bitcast(FP8X4), rhs_scale=grain_plane[a][:],
+                                    start=(a == 0), stop=(a == PASSES - 1))
+            if ear == "left":
+                nc.scalar.copy(out=h_slot[step], in_=acc[:])
+            else:
+                nc.scalar.activation(out=h_slot[step], in_=acc[:], func=ACT.Copy, scale=-1.0)
+
+        def scatter(step):
+            ear, b, t = steps[step]
+            page, places, gain = ((page_left[t], left_list, gain_left) if ear == "left"
+                                  else (page_right[t], right_list, gain_right))
+            nc.vector.tensor_tensor(page[:].indirect(places[:]), h_slot[step], gain[:, S * t:S * (t + 1)], MULT)
+
+        def make_left_rows(b, t):
+            nc.scalar.activation(out=left_rows[:, T2 * t:T2 * (t + 1)], in_=page_left[t][:], func=ACT.Copy,
+                                 scale=loud_col[:, b, t:t + 1])
+
+        def make_cosine(b, t, first, last):
+            def add_turned(half, term, start, stop):
+                for blk in range(4):
+                    m0 = BANK * half + P * blk
+                    nc.tensor.matmul(out=bank[2 + 2 * (t % 2) + half][:, P * blk:P * (blk + 1)], lhsT=term[:, m0:m0 + P],
+                                     rhs=ident[:], is_transpose=True, start=(start and blk == 0), stop=(stop and blk == 3))
+
+            for half in range(2):
+                add_turned(half, delay_rows[t], True, False)
+                add_turned(half, first, False, False)
+            for half in range(2):
+                add_turned(half, last, False, True)
+            for half in range(2):
+                arg = bank[2 + 2 * (t % 2) + half]
+                dst = cosine[b][:].rearrange("p (blk t c) -> p blk t c", t=PACK, c=P)[:, 4 * half:4 * half + 4, t, :]
+                nc.scalar.activation(out=dst, in_=arg[:].rearrange("p (blk c) -> p blk c", c=P), func=ACT.Abs)
+                nc.scalar.activation(out=dst, in_=dst, func=ACT.Sin, scale=-1.0, bias=math.pi / 2)
+
+        def quantise_left(b):
+            for half in range(2):
+                part = woven_left[:, PACK * BANK * half:PACK * BANK * (half + 1)] if b == 0 else grouped[half][:]
+                nc.scalar.copy(
+                    out=part.rearrange("p (c i t) -> p c t i", i=4, t=PACK),
+                    in_=left_rows[:].rearrange("p (t c i) -> p c t i", t=PACK, i=4)[:, P * half:P * (half + 1), :, :])
+                cols = slice(BANK * half, BANK * (half + 1))
+                nc.vector.quantize_mx(out=left_codes[b][:, cols].bitcast(FP8X4), scales=left_plane[b][:, cols], in_=part)
+
+        def weave_z(b, blocks):
+            for blk in blocks:
+                back = bank[6 + blk % 2] if b == 0 else bank[(2, 3, 6, 7)[blk % 4]]
+                for t in range(PACK):
+                    c0 = BANK * blk + P * t
+                    nc.tensor.transpose(back[:, P * t:P * (t + 1)], cosine[b][:, c0:c0 + P], ident[:])
+                nc.vector.tensor_tensor(
+                    out=woven_z[:, BANK * blk:BANK * (blk + 1)].rearrange("p (m t) -> p m t", t=PACK),
+                    in0=back[:].rearrange("p (t m) -> p m t", t=PACK),
+                    in1=tune_col[:, b, :].unsqueeze(1).to_broadcast([P, P, PACK]), op=MULT)
+
+        def quantise_z(b, m0, m1):
+            nc.vector.quantize_mx(out=z_codes[b][:, m0:m1].bitcast(FP8X4), scales=z_plane[b][:, m0:m1],
+                                  in_=woven_z[:, PACK * m0:PACK * m1])
+
+        sums = {(0, 0): bank[0], (1, 0): bank[1], (0, 1): bank[4], (1, 1): bank[5]}
+
+        def second(nt, m0, m1, weight, b, start, stop):
+            cols = slice(m0, m1)
+            acc = sums[(nt, m0 // BANK)][:, m0 % BANK:m0 % BANK + m1 - m0]
+            if weight == "w4":
+                lhs, lhs_plane = w4_codes[:, b, P * nt:P * (nt + 1)], w4_plane[:, b, P * nt:P * (nt + 1)]
+                rhs, rhs_plane = left_codes[b][:, cols], left_plane[b][:, cols]
+            else:
+                wc = slice(N * b + P * nt, N * b + P * (nt + 1))
+                lhs, lhs_plane = w3_codes[:, wc], w3_plane[:, wc]
+                rhs, rhs_plane = z_codes[b][:, cols], z_plane[b][:, cols]
+            nc.tensor.matmul_mx(out=acc, lhsT=lhs.bitcast(FP8X4), lhsT_scale=lhs_plane,
+                                rhs=rhs.bitcast(FP8X4), rhs_scale=rhs_plane, start=start, stop=stop)
+
+        steps = ([("right", 0, 0), ("right", 0, 1), ("right", 0, 2), ("left", 0, 0), ("right", 0, 3)]
+                 + [("left", 0, t) for t in range(1, PACK)]
+                 + [("left", 1, t) for t in range(PACK)] + [("right", 1, t) for t in range(PACK)])
+
+        phases(0)
+        phases(1)
+        for a in range(PASSES):
+            quantise_w1(a, 0)
+        for step in range(2, 5):
+            phases(step)
+        for a in range(PASSES):
+            quantise_w1(a, 1)
+        for step in range(5, 8):
+            phases(step)
+        for step in range(len(steps)):
+            scatter(step)
+            ear, b, t = steps[step]
+            if ear == "left" and b == 0:
+                make_cosine(0, t, page_right[t], page_left[t])
+                make_left_rows(0, t)
+                load_delay(1, t)
+                if t == 0:
+                    quantise_w3()
+                    for later in range(8, 12):
+                        phases(later)
+                if t == PACK - 1:
+                    phases(12)
+                    phases(13)
+                    quantise_left(0)
+                    phases(14)
+                    weave_z(0, range(0, 4))
+                    quantise_z(0, 0, BANK)
+                    weave_z(0, range(4, 6))
+            if ear == "left" and b == 1:
+                make_left_rows(1, t)
+                if t == PACK - 1:
+                    phases(15)
+                    quantise_left(1)
+                    for nt in range(2):
+                        second(nt, 0, BANK, "w4", 0, True, False)
+                        second(nt, 0, BANK, "w3", 0, False, False)
+            if ear == "right" and b == 1:
+                make_cosine(1, t, page_left[t], page_right[t])
+
+        def store(nt, half, on_vector):
+            result = result_slot[2 * half + nt]
+            if on_vector:
+                nc.vector.tensor_copy(out=result, in_=sums[(nt, half)][:])
+            else:
+                nc.scalar.copy(out=result, in_=sums[(nt, half)][:])
+            nc.sync.dma_start(out=out[P * nt:P * (nt + 1), BANK * half:BANK * (half + 1)], in_=result)
+
+        weave_z(0, range(6, 8))
+        quantise_z(0, BANK, T2)
+        weave_z(1, range(0, 4))
+        quantise_z(1, 0, BANK)
+        for nt in range(2):
+            second(nt, 0, BANK, "w3", 1, False, False)
+            second(nt, 0, BANK, "w4", 1, False, True)
+            store(nt, 0, False)
+        quarter = BANK // 2
+        weave_z(1, range(4, 6))
+        quantise_z(1, BANK, BANK + quarter)
+        for nt in range(2):
+            second(nt, BANK, T2, "w4", 0, True, False)
+            second(nt, BANK, BANK + quarter, "w3", 1, False, False)
+            second(nt, BANK, T2, "w3", 0, False, False)
+            second(nt, BANK, T2, "w4", 1, False, False)
+        weave_z(1, range(6, 8))
+        quantise_z(1, BANK + quarter, T2)
+        for nt in range(2):
+            second(nt, BANK + quarter, T2, "w3", 1, False, True)
+            store(nt, 1, nt == 1)

@@ -76,9 +76,9 @@ def tile_list_owl_phase_cosine_kernel(tc, tab_words, tab_scales, offs, offs2, of
         w3_codes = keep.tile([P, PASSES * N], U32, align_bytes=64)
         w3_plane = keep.tile([P, PASSES * N], U8, align_bytes=64)
         w4_codes = keep.tile([P, PASSES, N], U32, align_bytes=64)
-        left_rows = keep.tile([P, PACK * T2], BF16)
+        left_first = keep.tile([P, PACK * T2], BF16)
         woven_left = keep.tile([P, PACK * T2], BF16, align_bytes=64)
-        woven_z = keep.tile([P, PACK * T2], BF16, align_bytes=64)
+        woven_z = keep.tile([P, PACK * T2 + BANK], BF16, align_bytes=64)
         left_codes = [keep.tile([P, T2], U32, name="left_codes%d" % b, align_bytes=64) for b in range(PASSES)]
         left_plane = [keep.tile([P, T2], U8, name="left_plane%d" % b, align_bytes=64) for b in range(PASSES)]
         z_codes = [keep.tile([P, T2], U32, name="z_codes%d" % b, align_bytes=64) for b in range(PASSES)]
@@ -94,7 +94,8 @@ def tile_list_owl_phase_cosine_kernel(tc, tab_words, tab_scales, offs, offs2, of
 
         h_slot = ([slot(spare, 0), slot(spare, 1)] + [slot(stage[1], i) for i in range(3)]
                   + [slot(stage[2], i) for i in range(3)] + [slot(stage[0], i) for i in range(4)]
-                  + [slot(stage[1], 3), slot(stage[2], 3), slot(spare, 0), woven_z[:, 6 * BANK:8 * BANK].bitcast(F32)])
+                  + [slot(spare, 0), slot(spare, 1), slot(stage[2], 3), woven_z[:, 7 * BANK:9 * BANK].bitcast(F32)])
+        left_rows = [left_first[:], stage[1][:].bitcast(BF16)]
         result_slot = [slot(stage[0], i) for i in range(4)]
 
         nc.vector.memset(tab_plane[:].bitcast(I32), 0)
@@ -121,13 +122,15 @@ def tile_list_owl_phase_cosine_kernel(tc, tab_words, tab_scales, offs, offs2, of
             nc.sync.dma_start(out=w2_raw[b][:].bitcast(I32),
                               in_=w2_words[:, :, 2 * PASS * b:2 * PASS * (b + 1)].bitcast(I32).rearrange("a p w -> p a w"))
 
+        def load_tab(a):
+            nc.sync.dma_start(out=tab[a][:].bitcast(I32), in_=tab_words[a].rearrange("p t i -> p (t i)").bitcast(I32))
+
+        load_w2(0)
         nc.sync.dma_start(grain_list[:], offs)
         load_scale_rows(tab_plane, tab_scales)
-        load_w2(0)
+        load_tab(0)
         load_scale_rows(w2_plane_raw, w2_scales)
-        for a in range(PASSES):
-            nc.sync.dma_start(out=tab[a][:].bitcast(I32),
-                              in_=tab_words[a].rearrange("p t i -> p (t i)").bitcast(I32))
+        load_tab(1)
         load_w2(1)
         nc.sync.dma_start(right_list[:], offs3)
         load_gains(gain_right, wg2, 0)
@@ -178,7 +181,7 @@ def tile_list_owl_phase_cosine_kernel(tc, tab_words, tab_scales, offs, offs2, of
                                in_=w3_raw[:, cols].rearrange("p (j c i) -> p c j i", j=PACK, i=4))
             nc.vector.quantize_mx(out=w3_codes[:].bitcast(FP8X4), scales=w3_plane[:], in_=woven_z[:, 0:PACK * PASSES * N])
 
-        phase_bank = [0, 1, 0, 1, 1, 0, 6, 1, 7, 0, 6, 1, 4, 5, 4, 5]
+        phase_bank = [0, 1, 0, 1, 1, 0, 6, 1, 7, 0, 1, 0, 1, 0, 1, 0]
 
         def phases(step):
             ear, b, t = steps[step]
@@ -205,40 +208,47 @@ def tile_list_owl_phase_cosine_kernel(tc, tab_words, tab_scales, offs, offs2, of
             nc.vector.tensor_tensor(page[:].indirect(places[:]), h_slot[step], gain[:, S * t:S * (t + 1)], MULT)
 
         def make_left_rows(b, t):
-            nc.scalar.activation(out=left_rows[:, T2 * t:T2 * (t + 1)], in_=page_left[t][:], func=ACT.Copy,
-                                 scale=loud_col[:, b, t:t + 1])
+            width = BANK if t == PACK - 1 else T2
+            for m0 in range(0, T2, width):
+                nc.scalar.activation(out=left_rows[b][:, T2 * t + m0:T2 * t + m0 + width], in_=page_left[t][:, m0:m0 + width],
+                                     func=ACT.Copy, scale=loud_col[:, b, t:t + 1])
 
-        def make_cosine(b, t, first, last):
+        def make_cosine(b, t, first, last, banks, pieces):
             def add_turned(half, term, start, stop):
                 for blk in range(4):
                     m0 = BANK * half + P * blk
-                    nc.tensor.matmul(out=bank[2 + 2 * (t % 2) + half][:, P * blk:P * (blk + 1)], lhsT=term[:, m0:m0 + P],
+                    nc.tensor.matmul(out=bank[banks[half]][:, P * blk:P * (blk + 1)], lhsT=term[:, m0:m0 + P],
                                      rhs=ident[:], is_transpose=True, start=(start and blk == 0), stop=(stop and blk == 3))
 
             for half in range(2):
                 add_turned(half, delay_rows[t], True, False)
                 add_turned(half, first, False, False)
-            for half in range(2):
+            for half in (1, 0):
                 add_turned(half, last, False, True)
-            for half in range(2):
-                arg = bank[2 + 2 * (t % 2) + half]
+            for half in (1, 0):
+                arg = bank[banks[half]][:].rearrange("p (blk c) -> p blk c", c=P)
                 dst = cosine[b][:].rearrange("p (blk t c) -> p blk t c", t=PACK, c=P)[:, 4 * half:4 * half + 4, t, :]
-                nc.scalar.activation(out=dst, in_=arg[:].rearrange("p (blk c) -> p blk c", c=P), func=ACT.Abs)
-                nc.scalar.activation(out=dst, in_=dst, func=ACT.Sin, scale=-1.0, bias=math.pi / 2)
+                width = 4 // pieces
+                for i in range(pieces):
+                    blks = slice(width * i, width * (i + 1))
+                    nc.scalar.activation(out=dst[:, blks, :], in_=arg[:, blks, :], func=ACT.Abs)
+                for i in range(pieces):
+                    blks = slice(width * i, width * (i + 1))
+                    nc.scalar.activation(out=dst[:, blks, :], in_=dst[:, blks, :], func=ACT.Sin, scale=-1.0, bias=math.pi / 2)
 
-        def quantise_left(b):
-            for half in range(2):
+        def quantise_left(b, halves):
+            for half in halves:
                 part = woven_left[:, PACK * BANK * half:PACK * BANK * (half + 1)] if b == 0 else grouped[half][:]
                 nc.scalar.copy(
                     out=part.rearrange("p (c i t) -> p c t i", i=4, t=PACK),
-                    in_=left_rows[:].rearrange("p (t c i) -> p c t i", t=PACK, i=4)[:, P * half:P * (half + 1), :, :])
+                    in_=left_rows[b].rearrange("p (t c i) -> p c t i", t=PACK, i=4)[:, P * half:P * (half + 1), :, :])
                 cols = slice(BANK * half, BANK * (half + 1))
                 nc.vector.quantize_mx(out=left_codes[b][:, cols].bitcast(FP8X4), scales=left_plane[b][:, cols], in_=part)
 
         def weave_z(b, blocks):
             for blk in blocks:
-                back = bank[6 + blk % 2] if b == 0 else bank[(2, 3, 6, 7)[blk % 4]]
-                for t in range(PACK):
+                back = bank[6 + (blk + (1 if blk < 4 else 0)) % 2] if b == 0 else bank[(6, 7, 3, 2)[blk % 4]]
+                for t in (range(PACK) if (b, blk) != (1, 5) else reversed(range(PACK))):
                     c0 = BANK * blk + P * t
                     nc.tensor.transpose(back[:, P * t:P * (t + 1)], cosine[b][:, c0:c0 + P], ident[:])
                 nc.vector.tensor_tensor(
@@ -267,8 +277,9 @@ def tile_list_owl_phase_cosine_kernel(tc, tab_words, tab_scales, offs, offs2, of
 
         steps = ([("right", 0, 0), ("right", 0, 1), ("right", 0, 2), ("left", 0, 0), ("right", 0, 3)]
                  + [("left", 0, t) for t in range(1, PACK)]
-                 + [("left", 1, t) for t in range(PACK)] + [("right", 1, t) for t in range(PACK)])
+                 + [(ear, 1, t) for t in range(PACK) for ear in ("left", "right")])
 
+        quarter = BANK // 2
         phases(0)
         phases(1)
         for a in range(PASSES):
@@ -283,31 +294,44 @@ def tile_list_owl_phase_cosine_kernel(tc, tab_words, tab_scales, offs, offs2, of
             scatter(step)
             ear, b, t = steps[step]
             if ear == "left" and b == 0:
-                make_cosine(0, t, page_right[t], page_left[t])
+                make_cosine(0, t, page_right[t], page_left[t], (4 - 2 * (t % 2), 5 - 2 * (t % 2)), 1)
                 make_left_rows(0, t)
                 load_delay(1, t)
                 if t == 0:
                     quantise_w3()
-                    for later in range(8, 12):
-                        phases(later)
+                if t < PACK - 1:
+                    phases(8 + t)
+                if t == PACK - 2:
+                    phases(11)
                 if t == PACK - 1:
                     phases(12)
-                    phases(13)
-                    quantise_left(0)
-                    phases(14)
+                    quantise_left(0, range(1, 2))
+                    weave_z(0, range(4, 6))
+                    quantise_z(0, BANK, BANK + quarter)
+                    weave_z(0, range(6, 7))
                     weave_z(0, range(0, 4))
                     quantise_z(0, 0, BANK)
-                    weave_z(0, range(4, 6))
             if ear == "left" and b == 1:
                 make_left_rows(1, t)
-                if t == PACK - 1:
+                if t == 0:
+                    quantise_left(0, range(0, 1))
+                if t == 1:
+                    phases(13)
+                if t == 2:
                     phases(15)
-                    quantise_left(1)
+                if t == PACK - 1:
+                    quantise_left(1, range(0, 1))
+            if ear == "right" and b == 1:
+                make_cosine(1, t, page_left[t], page_right[t], (4, 5) if t == 0 else (2, 3), 2 if t == PACK - 1 else 1)
+                if t == 1:
+                    phases(14)
+                    for nt in range(2):
+                        second(nt, BANK, T2, "w4", 0, True, False)
+                        second(nt, BANK, BANK + quarter, "w3", 0, False, False)
+                if t == 2:
                     for nt in range(2):
                         second(nt, 0, BANK, "w4", 0, True, False)
                         second(nt, 0, BANK, "w3", 0, False, False)
-            if ear == "right" and b == 1:
-                make_cosine(1, t, page_left[t], page_right[t])
 
         def store(nt, half, on_vector):
             result = result_slot[2 * half + nt]
@@ -317,24 +341,22 @@ def tile_list_owl_phase_cosine_kernel(tc, tab_words, tab_scales, offs, offs2, of
                 nc.scalar.copy(out=result, in_=sums[(nt, half)][:])
             nc.sync.dma_start(out=out[P * nt:P * (nt + 1), BANK * half:BANK * (half + 1)], in_=result)
 
-        weave_z(0, range(6, 8))
-        quantise_z(0, BANK, T2)
-        weave_z(1, range(0, 4))
-        quantise_z(1, 0, BANK)
+        weave_z(0, range(7, 8))
+        quantise_z(0, BANK + quarter, T2)
+        weave_z(1, range(4, 8))
+        quantise_z(1, BANK, T2)
+        quantise_left(1, range(1, 2))
         for nt in range(2):
-            second(nt, 0, BANK, "w3", 1, False, False)
-            second(nt, 0, BANK, "w4", 1, False, True)
-            store(nt, 0, False)
-        quarter = BANK // 2
-        weave_z(1, range(4, 6))
-        quantise_z(1, BANK, BANK + quarter)
+            second(nt, 0, BANK, "w4", 1, False, False)
         for nt in range(2):
-            second(nt, BANK, T2, "w4", 0, True, False)
-            second(nt, BANK, BANK + quarter, "w3", 1, False, False)
-            second(nt, BANK, T2, "w3", 0, False, False)
-            second(nt, BANK, T2, "w4", 1, False, False)
-        weave_z(1, range(6, 8))
-        quantise_z(1, BANK + quarter, T2)
+            second(nt, BANK, T2, "w3", 1, False, False)
+            second(nt, BANK + quarter, T2, "w3", 0, False, False)
+            second(nt, BANK, T2, "w4", 1, False, True)
+            store(nt, 1, False)
+        for part in range(2):
+            weave_z(1, range(2 * part, 2 * part + 2))
+            quantise_z(1, quarter * part, quarter * (part + 1))
+            for nt in range(2):
+                second(nt, quarter * part, quarter * (part + 1), "w3", 1, False, part == 1)
         for nt in range(2):
-            second(nt, BANK + quarter, T2, "w3", 1, False, True)
-            store(nt, 1, nt == 1)
+            store(nt, 0, nt == 1)

@@ -39,8 +39,8 @@ def tile_list_owl_phase_cosine_kernel(tc, tab_words, tab_scales, offs, offs2, of
                 nc.sync.dma_start(out=plane[32 * q:32 * q + 4, :, :].bitcast(I32),
                                   in_=rows[:, 4 * q:4 * q + 4, :].rearrange("a r w -> r a w"))
 
-        def load_gains(gains, wg, pair):
-            cols = slice(2 * S * pair, 2 * S * (pair + 1))
+        def load_gains(gains, wg, t0, t1):
+            cols = slice(S * t0, S * t1)
             rows = wg.rearrange("(q t) j -> q (t j)", t=PACK)[:, cols]
             for q in range(4):
                 nc.sync.dma_start(out=gains[32 * q:32 * q + 32, cols], in_=rows)
@@ -59,7 +59,7 @@ def tile_list_owl_phase_cosine_kernel(tc, tab_words, tab_scales, offs, offs2, of
         loud_col = keep.tile([P, PASSES, PACK], F32)
         stage = [keep.tile([P, PACK * PASS], F32, name="stage%d" % i) for i in range(3)]
         spare = keep.tile([P, 2 * S], F32)
-        cosine = [keep.tile([P, PACK * T2], F32, name="cosine%d" % b) for b in range(PASSES)]
+        cosine = [keep.tile([P, PACK * T2], F32, name="cosine%d" % b, align_bytes=64) for b in range(PASSES)]
         delay_rows = [keep.tile([P, T2], F32, name="delay_rows%d" % t) for t in range(PACK)]
         page_right = [keep.tile([P, T2], F32, name="page_right%d" % t) for t in range(PACK)]
         page_left = [keep.tile([P, T2], F32, name="page_left%d" % t) for t in range(PACK)]
@@ -78,7 +78,7 @@ def tile_list_owl_phase_cosine_kernel(tc, tab_words, tab_scales, offs, offs2, of
         w4_codes = keep.tile([P, PASSES, N], U32, align_bytes=64)
         left_first = keep.tile([P, PACK * T2], BF16)
         woven_left = keep.tile([P, PACK * T2], BF16, align_bytes=64)
-        woven_z = keep.tile([P, PACK * T2 + BANK], BF16, align_bytes=64)
+        woven_z = keep.tile([P, PACK * T2], BF16, align_bytes=64)
         left_codes = [keep.tile([P, T2], U32, name="left_codes%d" % b, align_bytes=64) for b in range(PASSES)]
         left_plane = [keep.tile([P, T2], U8, name="left_plane%d" % b, align_bytes=64) for b in range(PASSES)]
         z_codes = [keep.tile([P, T2], U32, name="z_codes%d" % b, align_bytes=64) for b in range(PASSES)]
@@ -92,9 +92,13 @@ def tile_list_owl_phase_cosine_kernel(tc, tab_words, tab_scales, offs, offs2, of
         def slot(tile, i):
             return tile[:, S * i:S * (i + 1)]
 
-        h_slot = ([slot(spare, 0), slot(spare, 1)] + [slot(stage[1], i) for i in range(3)]
-                  + [slot(stage[2], i) for i in range(3)] + [slot(stage[0], i) for i in range(4)]
-                  + [slot(spare, 0), slot(spare, 1), slot(stage[2], 3), woven_z[:, 7 * BANK:9 * BANK].bitcast(F32)])
+        def z_pair(i):
+            return woven_z[:, 2 * BANK * i:2 * BANK * (i + 1)].bitcast(F32)
+
+        h_slot = ([slot(spare, 0), slot(spare, 1)] + [slot(stage[1], 0), slot(cosine[1], 0), slot(cosine[1], 1)]
+                  + [slot(stage[2], i) for i in range(3)] + [slot(stage[0], i) for i in range(3)]
+                  + [z_pair(2), z_pair(0), z_pair(1), slot(stage[2], 3), z_pair(3)])
+        late_left = [grouped[0][:], cosine[0][:, 0:2 * S].bitcast(BF16)]
         left_rows = [left_first[:], stage[1][:].bitcast(BF16)]
         result_slot = [slot(stage[0], i) for i in range(4)]
 
@@ -102,11 +106,6 @@ def tile_list_owl_phase_cosine_kernel(tc, tab_words, tab_scales, offs, offs2, of
         nc.vector.memset(w2_plane_raw[:].bitcast(I32), 0)
         nc.vector.memset(warm[:], 0.0)
         nc.scalar.activation(out=warm[:], in_=warm[:], func=ACT.Sin)
-        for t in range(PACK):
-            nc.gpsimd.memset(page_right[t][:], 0.0)
-        make_identity(nc, ident[:])
-        for t in range(PACK):
-            nc.gpsimd.memset(page_left[t][:], 0.0)
         nc.gpsimd.memset(w4_plane[:].bitcast(I32), 0)
 
         def load_w1(a, b):
@@ -133,17 +132,18 @@ def tile_list_owl_phase_cosine_kernel(tc, tab_words, tab_scales, offs, offs2, of
         load_tab(1)
         load_w2(1)
         nc.sync.dma_start(right_list[:], offs3)
-        load_gains(gain_right, wg2, 0)
+        load_gains(gain_right, wg2, 0, 2)
         for a in range(PASSES):
             load_w1(a, 0)
-        load_gains(gain_right, wg2, 1)
+        load_gains(gain_right, wg2, 2, 3)
         load_w1(0, 1)
         nc.sync.dma_start(left_list[:], offs2)
-        load_gains(gain_left, wg1, 0)
+        load_gains(gain_left, wg1, 0, 1)
+        load_gains(gain_right, wg2, 3, 4)
+        load_gains(gain_left, wg1, 1, 4)
         load_w1(1, 1)
         nc.sync.dma_start(out=loud_col[:], in_=loud.rearrange("(a p t) -> p a t", a=PASSES, t=PACK))
         load_delay(0, 0)
-        load_gains(gain_left, wg1, 1)
         for t in range(1, PACK):
             load_delay(0, t)
         for a in range(PASSES):
@@ -154,20 +154,28 @@ def tile_list_owl_phase_cosine_kernel(tc, tab_words, tab_scales, offs, offs2, of
         nc.sync.dma_start(out=w4_codes[:].bitcast(I32), in_=w4_words.rearrange("a p c i -> p a (c i)").bitcast(I32))
         load_scale_rows(w4_plane, w4_scales)
 
-        def order_w2(b):
+        def order_w2_words(b, t0, t1):
             nc.vector.tensor_copy(
-                out=w2_codes[b][:].bitcast(U16).rearrange("p a (t m) -> p a t m", t=PACK),
-                in_=w2_raw[b][:].bitcast(U16).rearrange("p a (m t) -> p a t m", t=PACK))
-            nc.vector.tensor_copy(
+                out=w2_codes[b][:].bitcast(U16).rearrange("p a (t m) -> p a t m", t=PACK)[:, :, t0:t1, :],
+                in_=w2_raw[b][:].bitcast(U16).rearrange("p a (m t) -> p a t m", t=PACK)[:, :, t0:t1, :])
+
+        def order_w2_plane(b):
+            nc.gpsimd.tensor_copy(
                 out=w2_plane[b][:].rearrange("p a (t m) -> p a t m", t=PACK),
                 in_=w2_plane_raw[:, :, PASS * b:PASS * (b + 1)].rearrange("p a (m t) -> p a t m", t=PACK))
 
         for a in range(PASSES):
-            nc.vector.tensor_copy(grain_plane[a][:], tab_plane[:, a, :].indirect(grain_list[:]))
-        order_w2(0)
-        for a in range(PASSES):
             nc.vector.tensor_copy(grain_codes[a][:], tab[a][:].indirect(grain_list[:]))
-        order_w2(1)
+            nc.vector.tensor_copy(grain_plane[a][:], tab_plane[:, a, :].indirect(grain_list[:]))
+        for b in range(PASSES):
+            order_w2_words(b, 0, PACK)
+        for b in range(PASSES):
+            order_w2_plane(b)
+        for t in range(PACK):
+            nc.gpsimd.memset(page_right[t][:], 0.0)
+        make_identity(nc, ident[:])
+        for t in range(PACK):
+            nc.gpsimd.memset(page_left[t][:], 0.0)
 
         def quantise_w1(a, b):
             nc.scalar.copy(out=grouped[a][:].rearrange("p (t m j) -> p m t j", t=PACK, j=PACK),
@@ -181,7 +189,7 @@ def tile_list_owl_phase_cosine_kernel(tc, tab_words, tab_scales, offs, offs2, of
                                in_=w3_raw[:, cols].rearrange("p (j c i) -> p c j i", j=PACK, i=4))
             nc.vector.quantize_mx(out=w3_codes[:].bitcast(FP8X4), scales=w3_plane[:], in_=woven_z[:, 0:PACK * PASSES * N])
 
-        phase_bank = [0, 1, 0, 1, 1, 0, 6, 1, 7, 0, 1, 0, 1, 0, 1, 0]
+        phase_bank = [0, 1, 0, 1, 7, 0, 6, 1, 5, 0, 1, 0, 1, 0, 1, 0]
 
         def phases(step):
             ear, b, t = steps[step]
@@ -213,7 +221,7 @@ def tile_list_owl_phase_cosine_kernel(tc, tab_words, tab_scales, offs, offs2, of
                 nc.scalar.activation(out=left_rows[b][:, T2 * t + m0:T2 * t + m0 + width], in_=page_left[t][:, m0:m0 + width],
                                      func=ACT.Copy, scale=loud_col[:, b, t:t + 1])
 
-        def make_cosine(b, t, first, last, banks, pieces):
+        def make_cosine(b, t, first, last, banks, pieces, scratch):
             def add_turned(half, term, start, stop):
                 for blk in range(4):
                     m0 = BANK * half + P * blk
@@ -228,33 +236,42 @@ def tile_list_owl_phase_cosine_kernel(tc, tab_words, tab_scales, offs, offs2, of
             for half in (1, 0):
                 arg = bank[banks[half]][:].rearrange("p (blk c) -> p blk c", c=P)
                 dst = cosine[b][:].rearrange("p (blk t c) -> p blk t c", t=PACK, c=P)[:, 4 * half:4 * half + 4, t, :]
+                size = scratch[half].rearrange("p (blk c) -> p blk c", c=P) if half in scratch else dst
                 width = 4 // pieces
                 for i in range(pieces):
                     blks = slice(width * i, width * (i + 1))
-                    nc.scalar.activation(out=dst[:, blks, :], in_=arg[:, blks, :], func=ACT.Abs)
+                    nc.scalar.activation(out=size[:, blks, :], in_=arg[:, blks, :], func=ACT.Abs)
                 for i in range(pieces):
                     blks = slice(width * i, width * (i + 1))
-                    nc.scalar.activation(out=dst[:, blks, :], in_=dst[:, blks, :], func=ACT.Sin, scale=-1.0, bias=math.pi / 2)
+                    nc.scalar.activation(out=dst[:, blks, :], in_=size[:, blks, :], func=ACT.Sin, scale=-1.0, bias=math.pi / 2)
 
         def quantise_left(b, halves):
             for half in halves:
-                part = woven_left[:, PACK * BANK * half:PACK * BANK * (half + 1)] if b == 0 else grouped[half][:]
+                part = woven_left[:, PACK * BANK * half:PACK * BANK * (half + 1)] if b == 0 else late_left[half]
                 nc.scalar.copy(
                     out=part.rearrange("p (c i t) -> p c t i", i=4, t=PACK),
                     in_=left_rows[b].rearrange("p (t c i) -> p c t i", t=PACK, i=4)[:, P * half:P * (half + 1), :, :])
                 cols = slice(BANK * half, BANK * (half + 1))
                 nc.vector.quantize_mx(out=left_codes[b][:, cols].bitcast(FP8X4), scales=left_plane[b][:, cols], in_=part)
 
+        def back_bank(b, blk):
+            return bank[6 + blk % 2] if b == 0 else bank[(6, 7, 3, 2)[blk % 4]]
+
+        def turn_back(b, blk):
+            for t in (reversed(range(PACK)) if b == 1 and blk in (4, 5) else range(PACK)):
+                c0 = BANK * blk + P * t
+                nc.tensor.transpose(back_bank(b, blk)[:, P * t:P * (t + 1)], cosine[b][:, c0:c0 + P], ident[:])
+
+        def scale_z(b, blk):
+            nc.vector.tensor_tensor(
+                out=woven_z[:, BANK * blk:BANK * (blk + 1)].rearrange("p (m t) -> p m t", t=PACK),
+                in0=back_bank(b, blk)[:].rearrange("p (t m) -> p m t", t=PACK),
+                in1=tune_col[:, b, :].unsqueeze(1).to_broadcast([P, P, PACK]), op=MULT)
+
         def weave_z(b, blocks):
             for blk in blocks:
-                back = bank[6 + (blk + (1 if blk < 4 else 0)) % 2] if b == 0 else bank[(6, 7, 3, 2)[blk % 4]]
-                for t in (range(PACK) if (b, blk) != (1, 5) else reversed(range(PACK))):
-                    c0 = BANK * blk + P * t
-                    nc.tensor.transpose(back[:, P * t:P * (t + 1)], cosine[b][:, c0:c0 + P], ident[:])
-                nc.vector.tensor_tensor(
-                    out=woven_z[:, BANK * blk:BANK * (blk + 1)].rearrange("p (m t) -> p m t", t=PACK),
-                    in0=back[:].rearrange("p (t m) -> p m t", t=PACK),
-                    in1=tune_col[:, b, :].unsqueeze(1).to_broadcast([P, P, PACK]), op=MULT)
+                turn_back(b, blk)
+                scale_z(b, blk)
 
         def quantise_z(b, m0, m1):
             nc.vector.quantize_mx(out=z_codes[b][:, m0:m1].bitcast(FP8X4), scales=z_plane[b][:, m0:m1],
@@ -284,37 +301,47 @@ def tile_list_owl_phase_cosine_kernel(tc, tab_words, tab_scales, offs, offs2, of
         phases(1)
         for a in range(PASSES):
             quantise_w1(a, 0)
-        for step in range(2, 5):
-            phases(step)
-        for a in range(PASSES):
-            quantise_w1(a, 1)
+        phases(2)
+        quantise_w1(0, 1)
+        phases(3)
+        phases(4)
+        quantise_w1(1, 1)
         for step in range(5, 8):
             phases(step)
         for step in range(len(steps)):
             scatter(step)
             ear, b, t = steps[step]
+            if step == 11:
+                for blk in range(4, 6):
+                    scale_z(0, blk)
+                    turn_back(0, blk - 4)
+                quantise_z(0, BANK, BANK + quarter)
+            if step == 12:
+                for blk in range(0, 2):
+                    scale_z(0, blk)
+                    turn_back(0, blk + 2)
+            if step == 13:
+                for blk in range(2, 4):
+                    scale_z(0, blk)
+                    turn_back(0, blk + 4)
+                quantise_z(0, 0, BANK)
             if ear == "left" and b == 0:
-                make_cosine(0, t, page_right[t], page_left[t], (4 - 2 * (t % 2), 5 - 2 * (t % 2)), 1)
+                make_cosine(0, t, page_right[t], page_left[t], (4 - 2 * (t % 2), 5 - 2 * (t % 2)), 1, {})
                 make_left_rows(0, t)
                 load_delay(1, t)
                 if t == 0:
                     quantise_w3()
                 if t < PACK - 1:
                     phases(8 + t)
-                if t == PACK - 2:
-                    phases(11)
                 if t == PACK - 1:
-                    phases(12)
+                    phases(11)
                     quantise_left(0, range(1, 2))
-                    weave_z(0, range(4, 6))
-                    quantise_z(0, BANK, BANK + quarter)
-                    weave_z(0, range(6, 7))
-                    weave_z(0, range(0, 4))
-                    quantise_z(0, 0, BANK)
+                    turn_back(0, 4)
+                    turn_back(0, 5)
             if ear == "left" and b == 1:
                 make_left_rows(1, t)
                 if t == 0:
-                    quantise_left(0, range(0, 1))
+                    phases(12)
                 if t == 1:
                     phases(13)
                 if t == 2:
@@ -322,8 +349,14 @@ def tile_list_owl_phase_cosine_kernel(tc, tab_words, tab_scales, offs, offs2, of
                 if t == PACK - 1:
                     quantise_left(1, range(0, 1))
             if ear == "right" and b == 1:
-                make_cosine(1, t, page_left[t], page_right[t], (4, 5) if t == 0 else (2, 3), 2 if t == PACK - 1 else 1)
+                if t < PACK - 1:
+                    make_cosine(1, t, page_left[t], page_right[t], (4, 5) if t == 0 else (2, 3), 1,
+                                {1: slot(stage[1], t + 1)})
+                else:
+                    make_cosine(1, t, page_left[t], page_right[t], (2, 3), 2,
+                                {half: slot(cosine[0], half) for half in range(2)})
                 if t == 1:
+                    quantise_left(0, range(0, 1))
                     phases(14)
                     for nt in range(2):
                         second(nt, BANK, T2, "w4", 0, True, False)
@@ -341,7 +374,8 @@ def tile_list_owl_phase_cosine_kernel(tc, tab_words, tab_scales, offs, offs2, of
                 nc.scalar.copy(out=result, in_=sums[(nt, half)][:])
             nc.sync.dma_start(out=out[P * nt:P * (nt + 1), BANK * half:BANK * (half + 1)], in_=result)
 
-        weave_z(0, range(7, 8))
+        scale_z(0, 6)
+        scale_z(0, 7)
         quantise_z(0, BANK + quarter, T2)
         weave_z(1, range(4, 8))
         quantise_z(1, BANK, T2)

@@ -31,6 +31,7 @@ def tile_list_owl_phase_cosine_kernel(tc, tab_words, tab_scales, offs, offs2, of
     nc = tc.nc
     with ExitStack() as ctx:
         keep = ctx.enter_context(tc.tile_pool(name="keep", bufs=1))
+        shared = ctx.enter_context(tc.tile_pool(name="shared", bufs=1))
         psum = ctx.enter_context(tc.psum_pool(name="psum", bufs=1))
 
         def load_scale_rows(plane, scales):
@@ -51,7 +52,10 @@ def tile_list_owl_phase_cosine_kernel(tc, tab_words, tab_scales, offs, offs2, of
         tab_plane = keep.tile([P, PASSES, T], U8, align_bytes=64)
         w2_plane_raw = keep.tile([P, PASSES, H], U8, align_bytes=64)
         w4_plane = keep.tile([P, PASSES, N], U8, align_bytes=64)
-        w2_raw = [keep.tile([P, PASSES, 2 * PASS], U8, name="w2_raw%d" % b, align_bytes=64) for b in range(PASSES)]
+        w2_raw_first = keep.tile([P, PASSES, 2 * PASS], U8, align_bytes=64)
+        page_bytes = 4 * T2
+        w2_raw_wide = shared.tile([P, (PACK + 1) * page_bytes], U8, offset=0)
+        w2_raw = [w2_raw_first[:], w2_raw_wide[:, 0:PASSES * 2 * PASS].rearrange("p (a c) -> p a c", a=PASSES)]
         tab = [keep.tile([P, T], U32, name="tab%d" % a, align_bytes=64) for a in range(PASSES)]
         gain_right = keep.tile([P, PACK * S], F32)
         gain_left = keep.tile([P, PACK * S], F32)
@@ -61,8 +65,9 @@ def tile_list_owl_phase_cosine_kernel(tc, tab_words, tab_scales, offs, offs2, of
         spare = keep.tile([P, 2 * S], F32)
         cosine = [keep.tile([P, PACK * T2], F32, name="cosine%d" % b, align_bytes=64) for b in range(PASSES)]
         delay_rows = [keep.tile([P, T2], F32, name="delay_rows%d" % t) for t in range(PACK)]
-        page_right = [keep.tile([P, T2], F32, name="page_right%d" % t) for t in range(PACK)]
-        page_left = [keep.tile([P, T2], F32, name="page_left%d" % t) for t in range(PACK)]
+        page_right = [keep.tile([P, T2], F32, name="page_right%d" % t) for t in range(PACK - 1)]
+        page_right.append(shared.tile([P, T2], F32, name="page_right_last", offset=PACK * page_bytes))
+        page_left = [shared.tile([P, T2], F32, name="page_left%d" % t, offset=t * page_bytes) for t in range(PACK)]
         ident = keep.tile([P, P], F32)
         grain_codes = [keep.tile([P, S], U32, name="grain_codes%d" % a, align_bytes=64) for a in range(PASSES)]
         grain_plane = [keep.tile([P, S], U8, name="grain_plane%d" % a, align_bytes=64) for a in range(PASSES)]
@@ -106,7 +111,10 @@ def tile_list_owl_phase_cosine_kernel(tc, tab_words, tab_scales, offs, offs2, of
         nc.vector.memset(w2_plane_raw[:].bitcast(I32), 0)
         nc.vector.memset(warm[:], 0.0)
         nc.scalar.activation(out=warm[:], in_=warm[:], func=ACT.Sin)
-        nc.gpsimd.memset(w4_plane[:].bitcast(I32), 0)
+        for t in range(PACK - 1):
+            nc.vector.memset(page_right[t][:], 0.0)
+        nc.vector.memset(w4_plane[:].bitcast(I32), 0)
+        make_identity(nc, ident[:])
 
         def load_w1(a, b):
             nc.sync.dma_start(out=w1_raw[(a, b)].rearrange("p (j c) -> p j c", j=PACK),
@@ -118,7 +126,7 @@ def tile_list_owl_phase_cosine_kernel(tc, tab_words, tab_scales, offs, offs2, of
                 "(p t) m -> p t m", t=PACK)[:, t, :])
 
         def load_w2(b):
-            nc.sync.dma_start(out=w2_raw[b][:].bitcast(I32),
+            nc.sync.dma_start(out=w2_raw[b].bitcast(I32),
                               in_=w2_words[:, :, 2 * PASS * b:2 * PASS * (b + 1)].bitcast(I32).rearrange("a p w -> p a w"))
 
         def load_tab(a):
@@ -154,13 +162,8 @@ def tile_list_owl_phase_cosine_kernel(tc, tab_words, tab_scales, offs, offs2, of
         nc.sync.dma_start(out=w4_codes[:].bitcast(I32), in_=w4_words.rearrange("a p c i -> p a (c i)").bitcast(I32))
         load_scale_rows(w4_plane, w4_scales)
 
-        def order_w2_words(b, t0, t1):
-            nc.vector.tensor_copy(
-                out=w2_codes[b][:].bitcast(U16).rearrange("p a (t m) -> p a t m", t=PACK)[:, :, t0:t1, :],
-                in_=w2_raw[b][:].bitcast(U16).rearrange("p a (m t) -> p a t m", t=PACK)[:, :, t0:t1, :])
-
         def order_w2_plane(b):
-            nc.gpsimd.tensor_copy(
+            nc.vector.tensor_copy(
                 out=w2_plane[b][:].rearrange("p a (t m) -> p a t m", t=PACK),
                 in_=w2_plane_raw[:, :, PASS * b:PASS * (b + 1)].rearrange("p a (m t) -> p a t m", t=PACK))
 
@@ -168,13 +171,12 @@ def tile_list_owl_phase_cosine_kernel(tc, tab_words, tab_scales, offs, offs2, of
             nc.vector.tensor_copy(grain_codes[a][:], tab[a][:].indirect(grain_list[:]))
             nc.vector.tensor_copy(grain_plane[a][:], tab_plane[:, a, :].indirect(grain_list[:]))
         for b in range(PASSES):
-            order_w2_words(b, 0, PACK)
-        for b in range(PASSES):
+            nc.vector.tensor_copy(out=w2_codes[b][:].bitcast(U16).rearrange("p a (t m) -> p a t m", t=PACK),
+                                  in_=w2_raw[b].bitcast(U16).rearrange("p a (m t) -> p a t m", t=PACK))
             order_w2_plane(b)
-        for t in range(PACK):
-            nc.gpsimd.memset(page_right[t][:], 0.0)
-        make_identity(nc, ident[:])
-        for t in range(PACK):
+        nc.gpsimd.memset(page_left[0][:], 0.0)
+        nc.gpsimd.memset(page_right[PACK - 1][:], 0.0)
+        for t in range(1, PACK):
             nc.gpsimd.memset(page_left[t][:], 0.0)
 
         def quantise_w1(a, b):

import math
from contextlib import ExitStack

import concourse.mybir as mybir
from concourse.masks import make_identity

K, H, N, T, S, T2 = 1024, 1024, 256, 2048, 512, 1024
FLOPS = 2 * (2 * K * H * S + 2 * H * N * T2)

F32 = mybir.dt.float32
BF16 = mybir.dt.bfloat16
I32 = mybir.dt.int32
U32 = mybir.dt.uint32
U16 = mybir.dt.uint16
U8 = mybir.dt.uint8
FP8X4 = mybir.dt.float8_e4m3fn_x4
FP4X4 = mybir.dt.float4_e2m1fn_x4
MULT = mybir.AluOpType.mult
ACT = mybir.ActivationFunctionType

P = 128
PACK = 4
PASS = P * PACK
PASSES = 2
BANK = 512
AHEAD = 4


def tile_list_owl_phase_cosine_kernel(tc, tab_words, tab_scales, offs, offs2, offs3, w1, w2_words, w2_scales,
                                                wg1, wg2, delay, tune, loud, w3, w4_words, w4_scales, out):
    nc = tc.nc
    with ExitStack() as ctx:
        keep = ctx.enter_context(tc.tile_pool(name="keep", bufs=1))
        shared = ctx.enter_context(tc.tile_pool(name="shared", bufs=1))
        psum = ctx.enter_context(tc.psum_pool(name="psum", bufs=1))

        def load_scale_rows(plane, scales):
            rows = scales.bitcast(I32)
            for q in range(4):
                nc.sync.dma_start(out=plane[32 * q:32 * q + 4, :, :].bitcast(I32),
                                  in_=rows[:, 4 * q:4 * q + 4, :].rearrange("a r w -> r a w"))

        def load_gains(gains, wg, t0, t1):
            cols = slice(S * t0, S * t1)
            rows = wg.rearrange("(q t) j -> q (t j)", t=PACK)[:, cols]
            for q in range(4):
                nc.sync.dma_start(out=gains[32 * q:32 * q + 32, cols], in_=rows)

        grain_list = keep.tile([P, S // 16], U16)
        left_list = keep.tile([P, S // 16], U16)
        right_list = keep.tile([P, S // 16], U16)
        tab_plane = keep.tile([P, PASSES, T], U8, align_bytes=64)
        w2_plane_raw = keep.tile([P, PASSES, H], U8, align_bytes=64)
        w4_plane = keep.tile([P, PASSES, N], U8, align_bytes=64)
        w2_raw_first = keep.tile([P, PASSES, 2 * PASS], U8, align_bytes=64)
        page_bytes = 4 * T2
        w2_raw_wide = shared.tile([P, (PACK + 1) * page_bytes], U8, offset=0)
        w2_raw = [w2_raw_first[:], w2_raw_wide[:, 0:PASSES * 2 * PASS].rearrange("p (a c) -> p a c", a=PASSES)]
        tab = [keep.tile([P, T], U32, name="tab%d" % a, align_bytes=64) for a in range(PASSES)]
        gain_right = keep.tile([P, PACK * S], F32)
        gain_left = keep.tile([P, PACK * S], F32)
        tune_col = keep.tile([P, PASSES, PACK], F32)
        loud_col = keep.tile([P, PASSES, PACK], F32)
        stage = [keep.tile([P, PACK * PASS], F32, name="stage%d" % i) for i in range(3)]
        spare = keep.tile([P, 2 * S], F32)
        cosine = [keep.tile([P, PACK * T2], F32, name="cosine%d" % b, align_bytes=64) for b in range(PASSES)]
        delay_rows = [keep.tile([P, T2], F32, name="delay_rows%d" % t) for t in range(PACK)]
        page_right = [keep.tile([P, T2], F32, name="page_right%d" % t) for t in range(PACK - 1)]
        page_right.append(shared.tile([P, T2], F32, name="page_right_last", offset=PACK * page_bytes))
        page_left = [shared.tile([P, T2], F32, name="page_left%d" % t, offset=t * page_bytes) for t in range(PACK)]
        ident = keep.tile([P, P], F32)
        grain_codes = [keep.tile([P, S], U32, name="grain_codes%d" % a, align_bytes=64) for a in range(PASSES)]
        grain_plane = [keep.tile([P, S], U8, name="grain_plane%d" % a, align_bytes=64) for a in range(PASSES)]
        w2_codes = [keep.tile([P, PASSES, 2 * PASS], U8, name="w2_codes%d" % b, align_bytes=64) for b in range(PASSES)]
        w2_plane = [keep.tile([P, PASSES, PASS], U8, name="w2_plane%d" % b, align_bytes=64) for b in range(PASSES)]
        grouped = [keep.tile([P, PACK * PASS], BF16, name="grouped%d" % a, align_bytes=64) for a in range(PASSES)]
        w1_codes = {(a, b): keep.tile([P, PASS], U32, name="w1_codes%d%d" % (a, b), align_bytes=64)
                    for a in range(PASSES) for b in range(PASSES)}
        w1_plane = {(a, b): keep.tile([P, PASS], U8, name="w1_plane%d%d" % (a, b), align_bytes=64)
                    for a in range(PASSES) for b in range(PASSES)}
        w3_codes = keep.tile([P, PASSES * N], U32, align_bytes=64)
        w3_plane = keep.tile([P, PASSES * N], U8, align_bytes=64)
        w4_codes = keep.tile([P, PASSES, N], U32, align_bytes=64)
        left_first = keep.tile([P, PACK * T2], BF16)
        woven_left = keep.tile([P, PACK * T2], BF16, align_bytes=64)
        woven_z = keep.tile([P, PACK * T2], BF16, align_bytes=64)
        left_codes = [keep.tile([P, T2], U32, name="left_codes%d" % b, align_bytes=64) for b in range(PASSES)]
        left_plane = [keep.tile([P, T2], U8, name="left_plane%d" % b, align_bytes=64) for b in range(PASSES)]
        z_codes = [keep.tile([P, T2], U32, name="z_codes%d" % b, align_bytes=64) for b in range(PASSES)]
        z_plane = [keep.tile([P, T2], U8, name="z_plane%d" % b, align_bytes=64) for b in range(PASSES)]
        warm = keep.tile([P, 1], F32)
        bank = [psum.tile([P, BANK], F32, name="bank%d" % i) for i in range(8)]

        w1_raw = {(0, 0): stage[0][:], (1, 0): stage[1][:], (0, 1): cosine[1][:, 0:PACK * PASS], (1, 1): stage[2][:]}
        w3_raw = cosine[1][:, PACK * PASS:2 * PACK * PASS]

        def slot(tile, i):
            return tile[:, S * i:S * (i + 1)]

        def z_pair(i):
            return woven_z[:, 2 * BANK * i:2 * BANK * (i + 1)].bitcast(F32)

        h_slot = ([slot(spare, 0), slot(spare, 1)] + [slot(stage[1], 0), slot(cosine[1], 0), slot(cosine[1], 1)]
                  + [slot(stage[2], i) for i in range(3)] + [slot(stage[0], i) for i in range(3)]
                  + [z_pair(2), z_pair(0), z_pair(1), slot(stage[2], 3), z_pair(3)])
        late_left = [grouped[0][:], cosine[0][:, 0:2 * S].bitcast(BF16)]
        left_rows = [left_first[:], stage[1][:].bitcast(BF16)]
        result_slot = [slot(stage[0], i) for i in range(4)]

        nc.vector.memset(tab_plane[:].bitcast(I32), 0)
        nc.vector.memset(w2_plane_raw[:].bitcast(I32), 0)
        nc.vector.memset(warm[:], 0.0)
        nc.scalar.activation(out=warm[:], in_=warm[:], func=ACT.Sin)
        for t in range(PACK - 1):
            nc.vector.memset(page_right[t][:], 0.0)
        nc.vector.memset(w4_plane[:].bitcast(I32), 0)
        make_identity(nc, ident[:])

        def load_w1(a, b):
            nc.sync.dma_start(out=w1_raw[(a, b)].rearrange("p (j c) -> p j c", j=PACK),
                              in_=w1[PASS * a:PASS * (a + 1), PASS * b:PASS * (b + 1)].rearrange(
                                  "(p j) c -> p j c", j=PACK))

        def load_delay(b, t):
            nc.sync.dma_start(out=delay_rows[t][:], in_=delay[PASS * b:PASS * (b + 1), :].rearrange(
                "(p t) m -> p t m", t=PACK)[:, t, :])

        def load_w2(b):
            nc.sync.dma_start(out=w2_raw[b].bitcast(I32),
                              in_=w2_words[:, :, 2 * PASS * b:2 * PASS * (b + 1)].bitcast(I32).rearrange("a p w -> p a w"))

        def load_tab(a):
            nc.sync.dma_start(out=tab[a][:].bitcast(I32), in_=tab_words[a].rearrange("p t i -> p (t i)").bitcast(I32))

        load_w2(0)
        nc.sync.dma_start(grain_list[:], offs)
        load_scale_rows(tab_plane, tab_scales)
        load_tab(0)
        load_scale_rows(w2_plane_raw, w2_scales)
        load_tab(1)
        load_w2(1)
        nc.sync.dma_start(right_list[:], offs3)
        load_gains(gain_right, wg2, 0, 2)
        for a in range(PASSES):
            load_w1(a, 0)
        load_gains(gain_right, wg2, 2, 3)
        load_w1(0, 1)
        nc.sync.dma_start(left_list[:], offs2)
        load_gains(gain_left, wg1, 0, 1)
        load_gains(gain_right, wg2, 3, 4)
        load_gains(gain_left, wg1, 1, 4)
        load_w1(1, 1)
        nc.sync.dma_start(out=loud_col[:], in_=loud.rearrange("(a p t) -> p a t", a=PASSES, t=PACK))
        load_delay(0, 0)
        for t in range(1, PACK):
            load_delay(0, t)
        for a in range(PASSES):
            nc.sync.dma_start(
                out=w3_raw[:, PACK * N * a:PACK * N * (a + 1)].rearrange("p (j n) -> p j n", j=PACK),
                in_=w3[PASS * a:PASS * (a + 1), :].rearrange("(p j) n -> p j n", j=PACK))
        nc.sync.dma_start(out=tune_col[:], in_=tune.rearrange("(a p t) -> p a t", a=PASSES, t=PACK))
        nc.sync.dma_start(out=w4_codes[:].bitcast(I32), in_=w4_words.rearrange("a p c i -> p a (c i)").bitcast(I32))
        load_scale_rows(w4_plane, w4_scales)

        def order_w2_plane(b):
            nc.vector.tensor_copy(
                out=w2_plane[b][:].rearrange("p a (t m) -> p a t m", t=PACK),
                in_=w2_plane_raw[:, :, PASS * b:PASS * (b + 1)].rearrange("p a (m t) -> p a t m", t=PACK))

        for a in range(PASSES):
            nc.vector.tensor_copy(grain_codes[a][:], tab[a][:].indirect(grain_list[:]))
            nc.vector.tensor_copy(grain_plane[a][:], tab_plane[:, a, :].indirect(grain_list[:]))
        for b in range(PASSES):
            nc.vector.tensor_copy(out=w2_codes[b][:].bitcast(U16).rearrange("p a (t m) -> p a t m", t=PACK),
                                  in_=w2_raw[b].bitcast(U16).rearrange("p a (m t) -> p a t m", t=PACK))
            order_w2_plane(b)
        nc.gpsimd.memset(page_left[0][:], 0.0)
        nc.gpsimd.memset(page_right[PACK - 1][:], 0.0)
        for t in range(1, PACK):
            nc.gpsimd.memset(page_left[t][:], 0.0)

        def quantise_w1(a, b):
            nc.scalar.copy(out=grouped[a][:].rearrange("p (t m j) -> p m t j", t=PACK, j=PACK),
                           in_=w1_raw[(a, b)].rearrange("p (j m t) -> p m t j", j=PACK, t=PACK))
            nc.vector.quantize_mx(out=w1_codes[(a, b)][:].bitcast(FP8X4), scales=w1_plane[(a, b)][:], in_=grouped[a][:])

        def quantise_w3():
            for a in range(PASSES):
                cols = slice(PACK * N * a, PACK * N * (a + 1))
                nc.scalar.copy(out=woven_z[:, cols].rearrange("p (c i j) -> p c j i", i=4, j=PACK),
                               in_=w3_raw[:, cols].rearrange("p (j c i) -> p c j i", j=PACK, i=4))
            nc.vector.quantize_mx(out=w3_codes[:].bitcast(FP8X4), scales=w3_plane[:], in_=woven_z[:, 0:PACK * PASSES * N])

        phase_bank = [0, 1, 0, 1, 7, 0, 6, 1, 5, 0, 1, 0, 1, 0, 1, 0]

        def phases(step):
            ear, b, t = steps[step]
            acc = bank[phase_bank[step]]
            cols = slice(P * t, P * (t + 1))
            for a in range(PASSES):
                if ear == "left":
                    lhs, lhs_plane = w1_codes[(a, b)][:, cols].bitcast(FP8X4), w1_plane[(a, b)][:, cols]
                else:
                    lhs = w2_codes[b][:, a, 2 * P * t:2 * P * (t + 1)].bitcast(FP4X4)
                    lhs_plane = w2_plane[b][:, a, cols]
                nc.tensor.matmul_mx(out=acc[:], lhsT=lhs, lhsT_scale=lhs_plane,
                                    rhs=grain_codes[a][:].bitcast(FP8X4), rhs_scale=grain_plane[a][:],
                                    start=(a == 0), stop=(a == PASSES - 1))
            if ear == "left":
                nc.scalar.copy(out=h_slot[step], in_=acc[:])
            else:
                nc.scalar.activation(out=h_slot[step], in_=acc[:], func=ACT.Copy, scale=-1.0)

        def scatter(step):
            ear, b, t = steps[step]
            page, places, gain = ((page_left[t], left_list, gain_left) if ear == "left"
                                  else (page_right[t], right_list, gain_right))
            nc.vector.tensor_tensor(page[:].indirect(places[:]), h_slot[step], gain[:, S * t:S * (t + 1)], MULT)

        def make_left_rows(b, t):
            width = BANK if t == PACK - 1 else T2
            for m0 in range(0, T2, width):
                nc.scalar.activation(out=left_rows[b][:, T2 * t + m0:T2 * t + m0 + width], in_=page_left[t][:, m0:m0 + width],
                                     func=ACT.Copy, scale=loud_col[:, b, t:t + 1])

        def make_cosine(b, t, first, last, banks, pieces, scratch):
            def add_turned(half, term, start, stop):
                for blk in range(4):
                    m0 = BANK * half + P * blk
                    nc.tensor.matmul(out=bank[banks[half]][:, P * blk:P * (blk + 1)], lhsT=term[:, m0:m0 + P],
                                     rhs=ident[:], is_transpose=True, start=(start and blk == 0), stop=(stop and blk == 3))

            for half in range(2):
                add_turned(half, delay_rows[t], True, False)
                add_turned(half, first, False, False)
            for half in (1, 0):
                add_turned(half, last, False, True)
            for half in (1, 0):
                arg = bank[banks[half]][:].rearrange("p (blk c) -> p blk c", c=P)
                dst = cosine[b][:].rearrange("p (blk t c) -> p blk t c", t=PACK, c=P)[:, 4 * half:4 * half + 4, t, :]
                size = scratch[half].rearrange("p (blk c) -> p blk c", c=P) if half in scratch else dst
                width = 4 // pieces
                for i in range(pieces):
                    blks = slice(width * i, width * (i + 1))
                    nc.scalar.activation(out=size[:, blks, :], in_=arg[:, blks, :], func=ACT.Abs)
                for i in range(pieces):
                    blks = slice(width * i, width * (i + 1))
                    nc.scalar.activation(out=dst[:, blks, :], in_=size[:, blks, :], func=ACT.Sin, scale=-1.0, bias=math.pi / 2)

        def quantise_left(b, halves):
            for half in halves:
                part = woven_left[:, PACK * BANK * half:PACK * BANK * (half + 1)] if b == 0 else late_left[half]
                nc.scalar.copy(
                    out=part.rearrange("p (c i t) -> p c t i", i=4, t=PACK),
                    in_=left_rows[b].rearrange("p (t c i) -> p c t i", t=PACK, i=4)[:, P * half:P * (half + 1), :, :])
                cols = slice(BANK * half, BANK * (half + 1))
                nc.vector.quantize_mx(out=left_codes[b][:, cols].bitcast(FP8X4), scales=left_plane[b][:, cols], in_=part)

        def back_bank(b, blk):
            return bank[6 + blk % 2] if b == 0 else bank[(6, 7, 3, 2)[blk % 4]]

        def turn_back(b, blk):
            for t in (reversed(range(PACK)) if b == 1 and blk in (4, 5) else range(PACK)):
                c0 = BANK * blk + P * t
                nc.tensor.transpose(back_bank(b, blk)[:, P * t:P * (t + 1)], cosine[b][:, c0:c0 + P], ident[:])

        def scale_z(b, blk):
            nc.vector.tensor_tensor(
                out=woven_z[:, BANK * blk:BANK * (blk + 1)].rearrange("p (m t) -> p m t", t=PACK),
                in0=back_bank(b, blk)[:].rearrange("p (t m) -> p m t", t=PACK),
                in1=tune_col[:, b, :].unsqueeze(1).to_broadcast([P, P, PACK]), op=MULT)

        def weave_z(b, blocks):
            for blk in blocks:
                turn_back(b, blk)
                scale_z(b, blk)

        def quantise_z(b, m0, m1):
            nc.vector.quantize_mx(out=z_codes[b][:, m0:m1].bitcast(FP8X4), scales=z_plane[b][:, m0:m1],
                                  in_=woven_z[:, PACK * m0:PACK * m1])

        sums = {(0, 0): bank[0], (1, 0): bank[1], (0, 1): bank[4], (1, 1): bank[5]}

        def second(nt, m0, m1, weight, b, start, stop):
            cols = slice(m0, m1)
            acc = sums[(nt, m0 // BANK)][:, m0 % BANK:m0 % BANK + m1 - m0]
            if weight == "w4":
                lhs, lhs_plane = w4_codes[:, b, P * nt:P * (nt + 1)], w4_plane[:, b, P * nt:P * (nt + 1)]
                rhs, rhs_plane = left_codes[b][:, cols], left_plane[b][:, cols]
            else:
                wc = slice(N * b + P * nt, N * b + P * (nt + 1))
                lhs, lhs_plane = w3_codes[:, wc], w3_plane[:, wc]
                rhs, rhs_plane = z_codes[b][:, cols], z_plane[b][:, cols]
            nc.tensor.matmul_mx(out=acc, lhsT=lhs.bitcast(FP8X4), lhsT_scale=lhs_plane,
                                rhs=rhs.bitcast(FP8X4), rhs_scale=rhs_plane, start=start, stop=stop)

        steps = ([("right", 0, 0), ("right", 0, 1), ("right", 0, 2), ("left", 0, 0), ("right", 0, 3)]
                 + [("left", 0, t) for t in range(1, PACK)]
                 + [(ear, 1, t) for t in range(PACK) for ear in ("left", "right")])

        quarter = BANK // 2
        phases(0)
        phases(1)
        for a in range(PASSES):
            quantise_w1(a, 0)
        phases(2)
        quantise_w1(0, 1)
        phases(3)
        phases(4)
        quantise_w1(1, 1)
        for step in range(5, 8):
            phases(step)
        for step in range(len(steps)):
            scatter(step)
            ear, b, t = steps[step]
            if step == 11:
                for blk in range(4, 6):
                    scale_z(0, blk)
                    turn_back(0, blk - 4)
                quantise_z(0, BANK, BANK + quarter)
            if step == 12:
                for blk in range(0, 2):
                    scale_z(0, blk)
                    turn_back(0, blk + 2)
            if step == 13:
                for blk in range(2, 4):
                    scale_z(0, blk)
                    turn_back(0, blk + 4)
                quantise_z(0, 0, BANK)
            if ear == "left" and b == 0:
                make_cosine(0, t, page_right[t], page_left[t], (4 - 2 * (t % 2), 5 - 2 * (t % 2)), 1, {})
                make_left_rows(0, t)
                load_delay(1, t)
                if t == 0:
                    quantise_w3()
                if t < PACK - 1:
                    phases(8 + t)
                if t == PACK - 1:
                    phases(11)
                    quantise_left(0, range(1, 2))
                    turn_back(0, 4)
                    turn_back(0, 5)
            if ear == "left" and b == 1:
                make_left_rows(1, t)
                if t == 0:
                    phases(12)
                if t == 1:
                    phases(13)
                if t == 2:
                    phases(15)
                if t == PACK - 1:
                    quantise_left(1, range(0, 1))
            if ear == "right" and b == 1:
                if t < PACK - 1:
                    make_cosine(1, t, page_left[t], page_right[t], (4, 5) if t == 0 else (2, 3), 1,
                                {1: slot(stage[1], t + 1)})
                else:
                    make_cosine(1, t, page_left[t], page_right[t], (2, 3), 2,
                                {half: slot(cosine[0], half) for half in range(2)})
                if t == 1:
                    quantise_left(0, range(0, 1))
                    phases(14)
                    for nt in range(2):
                        second(nt, BANK, T2, "w4", 0, True, False)
                        second(nt, BANK, BANK + quarter, "w3", 0, False, False)
                if t == 2:
                    for nt in range(2):
                        second(nt, 0, BANK, "w4", 0, True, False)
                        second(nt, 0, BANK, "w3", 0, False, False)

        def store(nt, half, on_vector):
            result = result_slot[2 * half + nt]
            if on_vector:
                nc.vector.tensor_copy(out=result, in_=sums[(nt, half)][:])
            else:
                nc.scalar.copy(out=result, in_=sums[(nt, half)][:])
            nc.sync.dma_start(out=out[P * nt:P * (nt + 1), BANK * half:BANK * (half + 1)], in_=result)

        scale_z(0, 6)
        scale_z(0, 7)
        quantise_z(0, BANK + quarter, T2)
        weave_z(1, range(4, 8))
        quantise_z(1, BANK, T2)
        quantise_left(1, range(1, 2))
        for nt in range(2):
            second(nt, 0, BANK, "w4", 1, False, False)
        for nt in range(2):
            second(nt, BANK, T2, "w3", 1, False, False)
            second(nt, BANK + quarter, T2, "w3", 0, False, False)
            second(nt, BANK, T2, "w4", 1, False, True)
            store(nt, 1, False)
        for part in range(2):
            weave_z(1, range(2 * part, 2 * part + 2))
            quantise_z(1, quarter * part, quarter * (part + 1))
            for nt in range(2):
                second(nt, quarter * part, quarter * (part + 1), "w3", 1, False, part == 1)
        for nt in range(2):
            store(nt, 0, nt == 1)
